import numpy as np
CORES = [0,1,2,3,4,5,6,7]
N = 8
ROOT = 5
WIDTHS = [1,1,4,2,2,4,4,1]
XW = 4
def setup_inputs(rng):
    return {"x": rng.standard_normal((N, 128, XW), dtype=np.float32)}
def reference(x):
    g = np.concatenate([x[r][:, :WIDTHS[r]] for r in range(N)], axis=1)
    y = np.full((N, 128, g.shape[1]), np.nan, x.dtype)
    y[ROOT] = g
    return {"y": y}

SCRATCH = {
    "land": ("sbuf", [128, 19], "float32"),
    "stage": ("sbuf", [128, 4], "float32"),
}
SEMAPHORES = ["loaded", "sent", "arrived", "stored"]

ROOT_RANK = 5


def rank_program(g, core, T, topo):
    rank = T.rank_of(core)
    if rank is None:
        return

    widths = T.tables["WIDTHS"]
    root_rank = ROOT_RANK if T.root is None else T.root
    root = T.cores[root_rank]
    off = sum(widths[:rank])
    w = widths[rank]
    total = sum(widths)

    if core != root:
        g.sync.dma_start(T.stage[:], T.x[:]).then_inc(T.sem.loaded, 16)
        g.wait_ge(T.sem.loaded, 16)
        rid, pid, _se = topo.addr(root)
        m = topo.mask(core, root)
        n_eng = bin(m).count("1")
        g.remote_dma(T.land[:, off:off + w], T.stage[:, 0:w],
                     remote_sem=T.sem.arrived, local_sem=T.sem.sent,
                     pid=pid, routing_id=rid, dma_engine_mask=m)
        g.wait_ge(T.sem.sent, n_eng)
        return

    if w == T.x.shape[1]:
        g.sync.dma_start(T.land[:, off:off + w], T.x[:]).then_inc(T.sem.loaded, 16)
        g.wait_ge(T.sem.loaded, 16)
    else:
        g.sync.dma_start(T.stage[:], T.x[:]).then_inc(T.sem.loaded, 16)
        g.sync.wait_ge(T.sem.loaded, 16)
        g.sync.dma_start(T.land[:, off:off + w], T.stage[:, 0:w]).then_inc(T.sem.loaded, 16)
        g.wait_ge(T.sem.loaded, 32)
    expected = sum(bin(topo.mask(c, root)).count("1") for c in T.cores if c != root)
    g.wait_ge(T.sem.arrived, expected)
    g.dma_start(T.y[:, 0:total], T.land[:, 0:total]).then_inc(T.sem.stored, 16)
    g.wait_ge(T.sem.stored, 16)
